import numpy as np, ml_dtypes
CORES = [83,85,87,115,117,119]
N = 6
import mx_ref
BF = ml_dtypes.bfloat16
def entries(a):
    return np.ascontiguousarray(a.T).reshape(-1)
def table(e):
    return np.ascontiguousarray(np.reshape(e, (-1, 16)).T).astype(np.int32)
def cols(t, e):
    v = np.concatenate([t.reshape(128, -1, 4), np.zeros((128, 1, 4), BF)], axis=1)
    return np.ascontiguousarray(v[:, e]).reshape(128, -1)
def cut(t, i, w=512):
    return t[:, w * i:w * i + w]
def f(rng, *shape):
    return mx_ref.flush((rng.standard_normal(shape, dtype=np.float32) * np.exp2(rng.integers(-2, 3, shape[:-1] + (1,)))).astype(BF))
def wide(rng, *shape, cols=0):
    v = rng.standard_normal(shape, dtype=np.float32) * np.exp2(rng.integers(-12, 13, shape)).astype(np.float32)
    if cols: v *= np.repeat(np.exp2(rng.integers(-cols, cols + 1, shape[:-2] + (1, shape[-1] // 4))) * (rng.random(shape[:-2] + (1, shape[-1] // 4)) > 0.0625), 4, axis=-1).astype(np.float32)
    return mx_ref.flush(v.astype(BF))
C, R, CAPP = 192, 3, 32
def lists(rng, full=False, stay=False, fresh=False, one=False):
    sl = np.full((N, R, N, CAPP), -1); pa = rng.integers(0, C, (N, R, C))
    for t in range(R):
        if stay: continue
        for r in range(N):
            for d in range(N):
                if d == r: continue
                n = CAPP if full else rng.integers(0, CAPP + 1)
                sl[r, t, d, rng.permutation(CAPP)[:n]] = rng.integers(0, C, n)
        for d in range(N):
            far = C + np.flatnonzero(sl[:, t, d].reshape(-1) >= 0)
            pa[d, t, rng.permutation(C)[:far.size]] = far
            if full: continue
            if far.size: pa[d, t, rng.integers(0, C, C // 16)] = rng.choice(far, C // 16)
            pa[d, t, rng.permutation(C)[:C // 2 if fresh else C // 8]] = -1
    if fresh: pa[rng.integers(0, N), rng.integers(0, R)] = -1
    if one:
        o, j = rng.integers(0, N), rng.integers(0, C)
        for t in range(R - 1):
            q, c, k = (o + rng.integers(1, N)) % N, rng.integers(0, CAPP), rng.integers(0, C)
            sl[o, t, q, c] = j; pa[q, t, k] = C + o * CAPP + c
            o, j = q, k
        for q in range(N):
            c = rng.integers(0, CAPP)
            if q != o: sl[o, R - 1, q, c] = j
            pa[q, R - 1] = j if q == o else C + o * CAPP + c
    return {"sl": np.stack([table(sl[r]) for r in range(N)]), "pa": np.stack([table(pa[r]) for r in range(N)])}
def setup_inputs(rng):
    return {"x": f(rng, N, 128, 4 * C * (R + 1)), "w": f(rng, N, 128, 512 * (R + 1)), **lists(rng)}
def setup_inputs_stay(rng):
    return {**setup_inputs(rng), **lists(rng, stay=True)}
def setup_inputs_far(rng):
    return {**setup_inputs(rng), **lists(rng, full=True)}
def setup_inputs_one(rng):
    return {**setup_inputs(rng), **lists(rng, one=True)}
def setup_inputs_fresh(rng):
    return {**setup_inputs(rng), **lists(rng, fresh=True)}
def setup_inputs_spread(rng):
    d = setup_inputs(rng); d["x"] = wide(rng, N, 128, 4 * C * (R + 1), cols=8); return d
def check_inputs(d):
    b = []
    s = [entries(d["sl"][r]).reshape(R, N, CAPP) for r in range(N)]
    for r in range(N):
        p = entries(d["pa"][r]).reshape(R, C)
        if s[r].min() < -1 or s[r].max() >= C or (s[r][:, r] != -1).any(): b.append("sl")
        if p.min() < -1 or p.max() >= C + N * CAPP: b.append("pa"); continue
        for t in range(R):
            slots = np.concatenate([s[q][t, r] for q in range(N)])
            if (slots[p[t][p[t] >= C] - C] < 0).any(): b.append("pa"); break
    return b
def reference(x, w, sl, pa):
    s = [entries(sl[r]).reshape(R, N, CAPP) for r in range(N)]
    p = [entries(pa[r]).reshape(R, C) for r in range(N)]
    cache = [np.ascontiguousarray(cut(x[r], 0, 4 * C)) for r in range(N)]
    y = np.zeros((N, 128, C * (R + 1)), np.float32)
    for t in range(R + 1):
        if t > 0:
            after = []
            for r in range(N):
                slots = [cols(cache[q], s[q][t - 1, r]) for q in range(N)]
                every = np.concatenate([cache[r]] + slots + [cut(x[r], t, 4 * C)], axis=1)
                v = p[r][t - 1]
                after.append(cols(every, np.where(v < 0, C + N * CAPP + np.arange(C), v)))
            cache = after
        for r in range(N):
            y[r][:, C * t:C * t + C] = mx_ref.matmul(mx_ref.quantize(np.ascontiguousarray(cut(w[r], t))), mx_ref.quantize(cache[r]))
    return {"y": y}

@@ -1,0 +1,369 @@
+from concourse.bass import DstId, RemoteDMATransfer
+from concourse.mybir import dt, AluOpType, ActivationFunctionType
+
+C, R, CAPP, N = 192, 3, 32, 6
+WIN = 3 * C
+NEW = 2 * C
+H = C // 16
+Q4 = 128 // 4
+MIN = 128
+BANK = 512
+PARTS = ("a", "b")
+CALLS = {1: (("q", "a"), ("s", "a"), ("q", "b"), ("s", "b"))}
+CALLS[2] = CALLS[3] = (("q", "a"), ("q", "b"), ("s", "a"), ("s", "b"))
+
+CODE, PLANE = "float8_e4m3fn_x4", "uint8"
+SCRATCH = {
+    "xb": ("sbuf", [128, 4 * C * (R + 1)], "bfloat16"),
+    "wb": ("sbuf", [128, 512 * (R + 1)], "bfloat16"),
+    "wq": ("sbuf", [128, 128 * (R + 1)], CODE), "ws": ("sbuf", [128, 128 * (R + 1)], PLANE),
+    "k0q": ("sbuf", [128, C], CODE), "k0s": ("sbuf", [128, C], PLANE),
+    "yb": ("sbuf", [128, C * (R + 1)], "float32"), "yw": ("sbuf", [128, WIN], "float32"),
+    "ps": ("psum", [128, BANK * 7], "float32"),
+    "rsl": ("sbuf", [128, 3 * H], "int32"), "rpa": ("sbuf", [128, 3 * H], "int32"),
+    "rsh": ("sbuf", [128, 2 * H], "int32"), "row": ("sbuf", [128, 2 * C], "int32"),
+    "xh": ("sbuf", [128, H], "int32"), "xa": ("sbuf", [128, H], "int32"),
+    "xd": ("sbuf", [128, H], "int32"), "xc": ("sbuf", [128, H], "int32"), "ox": ("sbuf", [128, 2 * H], "uint16"),
+    "tp": ("sbuf", [128, 2 * H], "float32"), "tn": ("sbuf", [128, 2 * H], "float32"),
+    "ioJ": ("sbuf", [128, 3 * H], "int32"), "ioK": ("sbuf", [128, 3 * H], "int32"),
+    "jl": ("sbuf", [128, 3 * H], "int32"), "jt": ("sbuf", [128, 3 * H], "int32"),
+    "pu": ("sbuf", [128, 3 * H], "int32"), "pr": ("sbuf", [128, 3 * H], "int32"),
+    "o1": ("sbuf", [128, H], "uint16"), "o2": ("sbuf", [128, H], "uint16"), "o3": ("sbuf", [128, H], "uint16"),
+    "po": ("sbuf", [128, 3 * H], "uint16"),
+}
+for _k in range(2):
+    SCRATCH["m%d" % _k] = ("sbuf", [128, C], "float32")
+    SCRATCH["z%d" % _k] = ("sbuf", [128, C], "float32")
+    for _n in ("u", "w"):
+        SCRATCH["c%s%d" % (_n, _k)] = ("sbuf", [128, H], "float32")
+for _t in range(R):
+    SCRATCH["win%dq" % _t] = ("sbuf", [128, WIN], CODE)
+    SCRATCH["win%ds" % _t] = ("sbuf", [128, WIN], PLANE)
+    SCRATCH["sn%dq" % (_t + 1)] = ("sbuf", [128, C], CODE)
+    SCRATCH["sn%ds" % (_t + 1)] = ("sbuf", [128, C], PLANE)
+
+SEMAPHORES = (["lx0", "lx1", "lx2", "lx3", "lw0", "lw2", "lsl", "ls2", "lsh", "lpa", "lrow", "st", "mz", "iot",
+               "va", "vb", "o1r", "o2r", "o3r", "por", "q0", "nw0", "nw1", "nw2", "qw0", "qw2", "lq1", "lq2", "left",
+               "kfq", "kfs", "anq", "ans", "ywr"]
+              + ["%s%d" % (n, t) for t in (1, 2, 3) for n in ("kq", "ks", "arq", "ars")]
+              + ["p%s%d%s" % (n, t, w) for t in (1, 2, 3) for n in "qs" for w in PARTS]
+              + ["mm%d" % t for t in range(7)] + ["yc%d" % t for t in range(4)])
+
+
+def peers(topo, cores, r):
+    ds = [d for d in range(len(cores)) if d != r]
+    home = topo.chip(cores[r])
+    return [d for d in ds if topo.chip(cores[d]) != home], [d for d in ds if topo.chip(cores[d]) == home]
+
+
+def bits(es):
+    return sum(1 << e for e in es)
+
+
+def parts_of(topo, cores, r, t):
+    off, on = peers(topo, cores, r)
+    return {"a": off, "b": on} if t == 1 else {"a": off[:2], "b": off[2:] + on}
+
+
+def engines_of(topo, cores, r, t):
+    off, on = peers(topo, cores, r)
+    far = topo.engines(cores[r], cores[off[0]])
+    near = [e for e in topo.engines(cores[r], cores[on[0]]) if e not in far]
+    h, q = len(far) // 2, len(far) // 4
+    a, b = far[:h], far[h:]
+    if t == 1:
+        plan = {off[0]: (a, b), off[1]: (b[:q], a[:q]), off[2]: (b[q:], a[q:])}
+    else:
+        plan = {off[0]: (a, a), off[1]: (b, b), off[2]: (far, far)}
+    k = len(near) // 2
+    for i, d in enumerate(on):
+        plan[d] = (near[i * k:i * k + k], near[i * k:i * k + k])
+    return plan
+
+
+def rank_program(g, core, T, topo):
+    r = T.rank_of(core)
+    if r is None:
+        return
+    S, V, A, Y = T.sem, g.vector, g.scalar, g.sync
+    cores = list(T.cores)
+    rounds = range(1, R + 1)
+    off, on = peers(topo, cores, r)
+    plan = {t: engines_of(topo, cores, r, t) for t in rounds}
+    to = {t: parts_of(topo, cores, r, t) for t in rounds}
+
+    def arrive(t, part, sources):
+        return sum(len(engines_of(topo, cores, q, t)[r]["qs".index(part)]) for q in sources)
+
+    order = to[2]["a"] + to[2]["b"]
+    at = {1: {d: CAPP * d for d in range(N)}}
+    at[2] = at[3] = {d: CAPP * i for i, d in enumerate(order)}
+    runs = []
+    for d in order:
+        if runs and runs[-1][0] + runs[-1][1] == d:
+            runs[-1][1] += 1
+        else:
+            runs.append([d, 1, at[2][d] // 16])
+
+    XP = 4 * C
+
+    def load_x(t):
+        Y.dma_start(T.xb[:, XP * t:XP * t + XP], T.x[:, XP * t:XP * t + XP]).then_inc(S["lx%d" % t], 16)
+
+    def load_w(a, b):
+        Y.dma_start(T.wb[:, 512 * a:512 * b], T.w[:, 512 * a:512 * b]).then_inc(S["lw%d" % a], 16)
+
+    def group(queue, buf, src, k, sem):
+        queue.dma_start(T[buf][16 * k:16 * k + 16, :], src[:, :]).then_inc(S[sem], 16)
+
+    def behind(t):
+        Y.wait_ge(S["lq%d" % t], sum(len(plan[t][d][0]) for d in to[t]["a"]))
+
+    load_x(0)
+    group(A, "rsl", T.sl, 0, "lsl")
+    group(A, "rsl", T.sl, 1, "lsl")
+    for k in range(8):
+        o = k % 2
+        A.dma_start(T.rsh[16 * k:16 * k + 16, 0:2 * H - o], T.sl[:, H + o:3 * H]).then_inc(S.lsh, 16)
+    Y.wait_ge(S.mz, 1)
+    for k in range(8):
+        Y.dma_start(T.row[16 * k:16 * k + 1, :], T.pa[:, 0:2 * H]).then_inc(S.lrow, 16)
+    for k in range(2, 8):
+        group(Y, "rsl", T.sl, k, "ls2")
+    load_x(1)
+    load_w(0, 2)
+    for k in range(8):
+        group(Y, "rpa", T.pa, k, "lpa")
+    load_x(2)
+    behind(1)
+    load_w(2, 4)
+    behind(2)
+    load_x(3)
+
+    g.iota(T.ioJ[:, :], [[0, 3 * H]], 0, 1).then_inc(S.iot, 1)
+    g.iota(T.ioK[:, :], [[0, R], [-16, H]], -NEW, 0).then_inc(S.iot, 1)
+
+    waits = 0
+    for t in rounds:
+        for part, where in CALLS[t]:
+            src, dst, i = T["sn%d%s" % (t, part)], T["win%d%s" % (t - 1, part)], "qs".index(part)
+            trs, n = [], 0
+            for d in to[t][where]:
+                rid, pid = topo.addr(cores[d])[:2]
+                a, b = at[t][d], C + CAPP * r
+                sv, dv = src[:, a:a + CAPP], dst[:, b:b + CAPP]
+                if part == "q":
+                    sv, dv = sv.bitcast(dt.uint8), dv.bitcast(dt.uint8)
+                sem = "an" + part if t == R and d in on else "ar%s%d" % (part, t)
+                trs.append(RemoteDMATransfer(dst_ids=[DstId(rid=rid, pnc=pid)], dma_engine_mask=bits(plan[t][d][i]),
+                                             remote_sem=S[sem], srcs=[sv], dsts=[dv]))
+                n += len(plan[t][d][i])
+            first = t < R and (part, where) == CALLS[t][0]
+            waits += 0 if first else n
+            g.wait_ge(S["p%s%d%s" % (part, t, where)], 1)
+            g.remote_dma_fused(trs, local_sem=S["lq%d" % t] if first else S.left)
+    g.wait_ge(S.left, waits)
+
+    n = {"va": 0, "vb": 0}
+
+    def step(chain, call):
+        call.then_inc(S[chain], 1)
+        n[chain] += 1
+
+    def need(chain):
+        V.wait_ge(S[chain], n[chain])
+
+    def pick(part, out, o, win, n_win, offs, w, sem):
+        if part == "q":
+            V.tensor_copy(T[out + "q"][:, o:o + w].bitcast(dt.uint32),
+                          T[win + "q"][:, 0:n_win].bitcast(dt.uint32).indirect(offs)).then_inc(S[sem], 1)
+        else:
+            A.activation(T[out + "s"][:, o:o + w], T[win + "s"][:, 0:n_win].indirect(offs), ActivationFunctionType.Copy).then_inc(S[sem], 1)
+
+    def pick_sends(part, t):
+        for w in PARTS:
+            a, b = min(at[t][d] for d in to[t][w]), max(at[t][d] for d in to[t][w]) + CAPP
+            pick(part, "sn%d" % t, a, "k0" if t == 1 else "win%d" % (t - 2), C if t == 1 else WIN,
+                 T["o%d" % t][:, a // 16:b // 16], b - a, "p%s%d%s" % (part, t, w))
+
+    def pick_cache(part, t):
+        pick(part, "win%d" % t, 0, "win%d" % (t - 1), WIN, T.po[:, H * (t - 1):H * t], C, "k%s%d" % (part, t))
+
+    def fill_own(part):
+        t = R - 1
+        pick(part, "win%d" % t, C + CAPP * r, "win%d" % (t - 1), WIN, T.po[:, H * (t - 1):H * (t - 1) + CAPP // 16], CAPP, "kf" + part)
+
+    def quantise(b, a, t, sem):
+        V.quantize_mx(T[b + "q"][:, a:a + C], T[b + "s"][:, a:a + C], T.xb[:, XP * t:XP * t + XP]).then_inc(S[sem], 1)
+
+    def quantise_w(a, b):
+        V.wait_ge(S["lw%d" % a], 16)
+        V.quantize_mx(T.wq[:, 128 * a:128 * b], T.ws[:, 128 * a:128 * b], T.wb[:, 512 * a:512 * b]).then_inc(S["qw%d" % a], 1)
+
+    V.memset(T.row[:, :], 0).then_inc(S.mz, 1)
+    V.wait_ge(S.lsl, 32)
+    for k in range(4):
+        V.tensor_copy(T.o1[Q4 * k:Q4 * k + Q4, :], T.rsl[0:32, 0:H]).then_inc(S.o1r, 1)
+    V.wait_ge(S.lx0, 16)
+    quantise("k0", 0, 0, "q0")
+    V.wait_ge(S.o1r, 4)
+    V.wait_ge(S.q0, 1)
+    pick_sends("q", 1)
+
+    def gather(k):
+        need("va")
+        step("va", V.tensor_copy(T["m%d" % k][:, :], T.row[:, :].indirect(T.ox[:, H * k:H * k + H])))
+
+    def turn(k):
+        need("va")
+        step("va", V.transpose(T["z%d" % k][:, :], T["m%d" % k][:, :]))
+
+    def fresh1(k):
+        need("va")
+        step("va", V.tensor_tensor(T["cu%d" % k][:, :], T["z%d" % k][:, 0:C:16], T.tn[:, H * k:H * k + H], AluOpType.mult))
+
+    def fresh2(k):
+        need("va")
+        step("va", V.tensor_tensor(T["cw%d" % k][:, :], T["cu%d" % k][:, :], T["z%d" % k][:, 0:C:16], AluOpType.max))
+
+    def offsets(k, out):
+        need("va")
+        for d, c, a in runs:
+            V.tensor_copy(T[out][:, a:a + 2 * c], T["cw%d" % k][:, 2 * d:2 * d + 2 * c]).then_inc(S[out + "r"], 1)
+
+    V.wait_ge(S.lsh, 128)
+    step("va", V.tensor_scalar(T.xh[:, :], T.rsh[:, 0:2 * H:2], 4, None, AluOpType.arith_shift_right))
+    for k in range(2):
+        step("va", V.tensor_scalar(T.xa[:, H // 2 * k:H // 2 * (k + 1)], T.rsh[:, H * k:H * k + H:2], 2 * H, H * k, AluOpType.mult, AluOpType.add))
+    V.wait_ge(S.ls2, 96)
+    step("vb", V.tensor_scalar(T.tp[:, :], T.rsl[:, H:3 * H], 0, NEW, AluOpType.max, AluOpType.add))
+    need("va")
+    step("va", V.tensor_scalar(T.xd[:, :], T.xh[:, :], 1 - 32 * H, None, AluOpType.mult))
+    quantise("win0", 0, 0, "nw0")
+    need("va")
+    step("va", V.tensor_tensor(T.xc[:, :], T.xa[:, :], T.xd[:, :], AluOpType.add))
+    need("vb")
+    step("vb", V.tensor_scalar(T.tn[:, :], T.tp[:, :], -1, None, AluOpType.mult))
+    need("va")
+    step("va", V.tensor_copy(T.ox[:, 0:2 * H:2], T.xc[:, :]))
+    step("va", V.tensor_copy(T.ox[:, 1:2 * H:2], T.xc[:, :]))
+    V.wait_ge(S.mz, 1)
+    V.wait_ge(S.lrow, 128)
+    gather(0)
+    V.wait_ge(S.lx1, 16)
+    quantise("win0", NEW, 1, "nw0")
+    turn(0)
+    need("vb")
+    fresh1(0)
+    fresh2(0)
+    offsets(0, "o2")
+
+    V.wait_ge(S.nw0, 2)
+    V.wait_ge(S.o2r, len(runs))
+    V.wait_ge(S.arq1, arrive(1, "q", off + on))
+    pick_sends("q", 2)
+    V.wait_ge(S.iot, 2)
+    step("vb", V.tensor_scalar(T.jl[:, :], T.ioJ[:, :], 15, None, AluOpType.bitwise_and))
+    gather(1)
+    need("vb")
+    step("vb", V.tensor_tensor(T.jt[:, :], T.ioK[:, :], T.jl[:, :], AluOpType.subtract))
+    turn(1)
+    V.wait_ge(S.lpa, 128)
+    need("vb")
+    step("vb", V.tensor_tensor(T.pu[:, :], T.rpa[:, :], T.jt[:, :], AluOpType.mult))
+    fresh1(1)
+    need("vb")
+    step("vb", V.tensor_tensor(T.pr[:, :], T.pu[:, :], T.rpa[:, :], AluOpType.max))
+    fresh2(1)
+    need("vb")
+    V.tensor_copy(T.po[:, :], T.pr[:, :]).then_inc(S.por, 1)
+    offsets(1, "o3")
+    V.wait_ge(S.por, 1)
+    pick_cache("q", 1)
+    V.wait_ge(S.lx2, 16)
+    quantise("win1", NEW, 2, "nw1")
+
+    V.wait_ge(S.kq1, 1)
+    V.wait_ge(S.nw1, 1)
+    V.wait_ge(S.o3r, len(runs))
+    V.wait_ge(S.arq2, arrive(2, "q", off + on))
+    pick_sends("q", 3)
+    pick_cache("q", 2)
+    fill_own("q")
+    quantise_w(0, 2)
+    quantise_w(2, 4)
+    V.wait_ge(S.lx3, 16)
+    quantise("win2", NEW, 3, "nw2")
+
+    home = sorted(on + [r])
+    regions = {4: (NEW, NEW, C), 5: None, 6: None}
+    for bank, ranks in ((5, home), (6, off)):
+        a = C + CAPP * ranks[0]
+        w = CAPP * len(ranks)
+        regions[bank] = (a - (MIN - w) if a == C else a, a, w)
+
+    for bank in (4, 5, 6):
+        s, a, w = regions[bank]
+        V.wait_ge(S["mm%d" % bank], 1)
+        V.tensor_copy(T.yw[:, a:a + w], T.ps[:, BANK * bank + a - s:BANK * bank + a - s + w]).then_inc(S.ywr, 1)
+    V.wait_ge(S.ywr, 4)
+    h = H * (R - 1)
+    V.tensor_copy(T.yb[:, R * C:R * C + C // 2], T.yw[:, :].indirect(T.po[:, h:h + H // 2])).then_inc(S.yc3, 1)
+
+    A.wait_ge(S.o1r, 4)
+    A.wait_ge(S.q0, 1)
+    pick_sends("s", 1)
+    A.wait_ge(S.nw0, 2)
+    A.wait_ge(S.o2r, len(runs))
+    A.wait_ge(S.ars1, arrive(1, "s", off + on))
+    pick_sends("s", 2)
+    A.wait_ge(S.por, 1)
+    pick_cache("s", 1)
+    A.wait_ge(S.ks1, 1)
+    A.wait_ge(S.nw1, 1)
+    A.wait_ge(S.o3r, len(runs))
+    A.wait_ge(S.ars2, arrive(2, "s", off + on))
+    pick_sends("s", 3)
+    pick_cache("s", 2)
+    fill_own("s")
+    for t in range(R):
+        A.wait_ge(S["mm%d" % t], 1)
+        A.activation(T.yb[:, C * t:C * t + C], T.ps[:, BANK * t:BANK * t + C], ActivationFunctionType.Copy).then_inc(S["yc%d" % t], 1)
+    A.wait_ge(S.mm3, 1)
+    A.activation(T.yw[:, 0:C], T.ps[:, BANK * 3:BANK * 3 + C], ActivationFunctionType.Copy).then_inc(S.ywr, 1)
+    A.wait_ge(S.ywr, 4)
+    A.activation(T.yb[:, R * C + C // 2:R * C + C], T.yw[:, :].indirect(T.po[:, h + H // 2:h + H]), ActivationFunctionType.Copy).then_inc(S.yc3, 1)
+
+    P = g.tensor
+
+    def product(bank, b, a, w):
+        t = min(bank, R)
+        P.matmul_mx(T.ps[:, BANK * bank:BANK * bank + w], T.wq[:, 128 * t:128 * t + 128], T.ws[:, 128 * t:128 * t + 128],
+                    T[b + "q"][:, a:a + w], T[b + "s"][:, a:a + w], True, True).then_inc(S["mm%d" % bank], 1)
+
+    P.wait_ge(S.q0, 1)
+    P.wait_ge(S.qw0, 1)
+    product(0, "k0", 0, C)
+    P.wait_ge(S.kq1, 1)
+    P.wait_ge(S.ks1, 1)
+    product(1, "win1", 0, C)
+    P.wait_ge(S.qw2, 1)
+    P.wait_ge(S.kq2, 1)
+    P.wait_ge(S.ks2, 1)
+    product(2, "win2", 0, C)
+    product(3, "win2", 0, C)
+    P.wait_ge(S.nw2, 1)
+    product(4, "win2", NEW, C)
+    P.wait_ge(S.kfq, 1)
+    P.wait_ge(S.kfs, 1)
+    P.wait_ge(S.anq, arrive(R, "q", on))
+    P.wait_ge(S.ans, arrive(R, "s", on))
+    product(5, "win2", regions[5][0], MIN)
+    P.wait_ge(S.arq3, arrive(R, "q", off))
+    P.wait_ge(S.ars3, arrive(R, "s", off))
+    product(6, "win2", regions[6][0], MIN)
+
+    for t in range(R + 1):
+        Y.wait_ge(S["yc%d" % t], 2 if t == R else 1)
+        Y.dma_start(T.y[:, C * t:C * t + C], T.yb[:, C * t:C * t + C]).then_inc(S.st, 16)
+    Y.wait_ge(S.st, 16 * (R + 1))

@@ -8,9 +8,6 @@ H = C // 16
 Q4 = 128 // 4
 MIN = 128
 BANK = 512
-PARTS = ("a", "b")
-CALLS = {1: (("q", "a"), ("s", "a"), ("q", "b"), ("s", "b"))}
-CALLS[2] = CALLS[3] = (("q", "a"), ("q", "b"), ("s", "a"), ("s", "b"))
 
 CODE, PLANE = "float8_e4m3fn_x4", "uint8"
 SCRATCH = {
@@ -21,32 +18,27 @@ SCRATCH = {
     "yb": ("sbuf", [128, C * (R + 1)], "float32"), "yw": ("sbuf", [128, WIN], "float32"),
     "ps": ("psum", [128, BANK * 7], "float32"),
     "rsl": ("sbuf", [128, 3 * H], "int32"), "rpa": ("sbuf", [128, 3 * H], "int32"),
-    "rsh": ("sbuf", [128, 2 * H], "int32"), "row": ("sbuf", [128, 2 * C], "int32"),
-    "xh": ("sbuf", [128, H], "int32"), "xa": ("sbuf", [128, H], "int32"),
-    "xd": ("sbuf", [128, H], "int32"), "xc": ("sbuf", [128, H], "int32"), "ox": ("sbuf", [128, 2 * H], "uint16"),
-    "tp": ("sbuf", [128, 2 * H], "float32"), "tn": ("sbuf", [128, 2 * H], "float32"),
+    "rsh": ("sbuf", [128, H], "int32"), "row": ("sbuf", [128, 256], "int32"),
+    "xa": ("sbuf", [128, H // 2], "int32"), "xc": ("sbuf", [128, H // 2], "int32"), "ox": ("sbuf", [128, H], "uint16"),
+    "tn": ("sbuf", [128, H], "float32"), "m": ("sbuf", [128, C], "float32"), "z": ("sbuf", [128, C], "float32"),
+    "cu": ("sbuf", [128, H], "float32"), "cw": ("sbuf", [128, H], "float32"),
     "ioJ": ("sbuf", [128, 3 * H], "int32"), "ioK": ("sbuf", [128, 3 * H], "int32"),
     "jl": ("sbuf", [128, 3 * H], "int32"), "jt": ("sbuf", [128, 3 * H], "int32"),
     "pu": ("sbuf", [128, 3 * H], "int32"), "pr": ("sbuf", [128, 3 * H], "int32"),
     "o1": ("sbuf", [128, H], "uint16"), "o2": ("sbuf", [128, H], "uint16"), "o3": ("sbuf", [128, H], "uint16"),
     "po": ("sbuf", [128, 3 * H], "uint16"),
 }
-for _k in range(2):
-    SCRATCH["m%d" % _k] = ("sbuf", [128, C], "float32")
-    SCRATCH["z%d" % _k] = ("sbuf", [128, C], "float32")
-    for _n in ("u", "w"):
-        SCRATCH["c%s%d" % (_n, _k)] = ("sbuf", [128, H], "float32")
 for _t in range(R):
     SCRATCH["win%dq" % _t] = ("sbuf", [128, WIN], CODE)
     SCRATCH["win%ds" % _t] = ("sbuf", [128, WIN], PLANE)
     SCRATCH["sn%dq" % (_t + 1)] = ("sbuf", [128, C], CODE)
     SCRATCH["sn%ds" % (_t + 1)] = ("sbuf", [128, C], PLANE)
 
-SEMAPHORES = (["lx0", "lx1", "lx2", "lx3", "lw0", "lw2", "lsl", "ls2", "lsh", "lpa", "lrow", "st", "mz", "iot",
-               "va", "vb", "o1r", "o2r", "o3r", "por", "q0", "nw0", "nw1", "nw2", "qw0", "qw2", "lq1", "lq2", "left",
+SEMAPHORES = (["lx0", "lx1", "lx2", "lx3", "lw0", "lw2", "lsl", "cpq", "cps", "lsh", "lpa", "lrow", "st", "mz", "iot",
+               "va", "vb", "o1r", "o2r", "o3r", "por", "q0", "nw0", "nw1", "nw2", "qw0", "qw2", "lq1", "lq3", "left",
                "kfq", "kfs", "anq", "ans", "ywr"]
               + ["%s%d" % (n, t) for t in (1, 2, 3) for n in ("kq", "ks", "arq", "ars")]
-              + ["p%s%d%s" % (n, t, w) for t in (1, 2, 3) for n in "qs" for w in PARTS]
+              + ["p%s%d%d" % (n, t, w) for t in (1, 2, 3) for n in "qs" for w in range(N - 1)]
               + ["mm%d" % t for t in range(7)] + ["yc%d" % t for t in range(4)])
 
 
@@ -60,25 +52,41 @@ def bits(es):
     return sum(1 << e for e in es)
 
 
-def parts_of(topo, cores, r, t):
-    off, on = peers(topo, cores, r)
-    return {"a": off, "b": on} if t == 1 else {"a": off[:2], "b": off[2:] + on}
+def share(ds, es):
+    k = len(es) // len(ds)
+    return {d: es[k * i:k * i + k] for i, d in enumerate(ds)}
 
 
-def engines_of(topo, cores, r, t):
+def lone(topo, cores, r):
+    return [(topo.chip(c), topo.die(c)) for c in cores].count((topo.chip(cores[r]), topo.die(cores[r]))) == 1
+
+
+def calls_of(topo, cores, r, t):
     off, on = peers(topo, cores, r)
     far = topo.engines(cores[r], cores[off[0]])
     near = [e for e in topo.engines(cores[r], cores[on[0]]) if e not in far]
-    h, q = len(far) // 2, len(far) // 4
-    a, b = far[:h], far[h:]
+    n = share(on, near)
+    i = sorted(on + [r]).index(r) + 1
+    off = off[i % len(off):] + off[:i % len(off)]
+    if t < R and not lone(topo, cores, r):
+        off.sort(key=lambda d: (lone(topo, cores, d), d))
+        off.insert(1, off.pop())
+    a, b, c = [{d: far} for d in off]
+    on.sort(key=lambda d: topo.die(cores[d]) == topo.die(cores[r]))
+    u, v = [{d: near} for d in on]
     if t == 1:
-        plan = {off[0]: (a, b), off[1]: (b[:q], a[:q]), off[2]: (b[q:], a[q:])}
-    else:
-        plan = {off[0]: (a, a), off[1]: (b, b), off[2]: (far, far)}
-    k = len(near) // 2
-    for i, d in enumerate(on):
-        plan[d] = (near[i * k:i * k + k], near[i * k:i * k + k])
-    return plan
+        if lone(topo, cores, r):
+            return [(part, to) for part in "qs" for to in (a, b, n, c)]
+        return [("q", to) for to in (a, b, c, n)] + [("s", to) for to in (b, c, a, n)]
+    if t < R and not lone(topo, cores, r):
+        return [("q", to) for to in (a, u, b, c, v)] + [("s", to) for to in (b, u, c, a, v)]
+    if t == R and r > max(on):
+        return [("q", a), ("q", u), ("q", b), ("q", v), ("s", a), ("q", c), ("s", u), ("s", b), ("s", c), ("s", v)]
+    return [(part, to) for part in "qs" for to in ((a, u, b, v, c) if lone(topo, cores, r) else (a, u, b, c, v))]
+
+
+def pieces_of(calls, t):
+    return [(min(to), max(to)) for part, to in calls if part == "q"]
 
 
 def rank_program(g, core, T, topo):
@@ -89,21 +97,11 @@ def rank_program(g, core, T, topo):
     cores = list(T.cores)
     rounds = range(1, R + 1)
     off, on = peers(topo, cores, r)
-    plan = {t: engines_of(topo, cores, r, t) for t in rounds}
-    to = {t: parts_of(topo, cores, r, t) for t in rounds}
+    calls = {t: calls_of(topo, cores, r, t) for t in rounds}
+    pieces = {t: pieces_of(calls[t], t) for t in rounds}
 
     def arrive(t, part, sources):
-        return sum(len(engines_of(topo, cores, q, t)[r]["qs".index(part)]) for q in sources)
-
-    order = to[2]["a"] + to[2]["b"]
-    at = {1: {d: CAPP * d for d in range(N)}}
-    at[2] = at[3] = {d: CAPP * i for i, d in enumerate(order)}
-    runs = []
-    for d in order:
-        if runs and runs[-1][0] + runs[-1][1] == d:
-            runs[-1][1] += 1
-        else:
-            runs.append([d, 1, at[2][d] // 16])
+        return sum(len(to[r]) for q in sources for p, to in calls_of(topo, cores, q, t) if p == part and r in to)
 
     XP = 4 * C
 
@@ -117,51 +115,56 @@ def rank_program(g, core, T, topo):
         queue.dma_start(T[buf][16 * k:16 * k + 16, :], src[:, :]).then_inc(S[sem], 16)
 
     def behind(t):
-        Y.wait_ge(S["lq%d" % t], sum(len(plan[t][d][0]) for d in to[t]["a"]))
+        Y.wait_ge(S["lq%d" % t], 1)
 
     load_x(0)
     group(A, "rsl", T.sl, 0, "lsl")
     group(A, "rsl", T.sl, 1, "lsl")
-    for k in range(8):
-        o = k % 2
-        A.dma_start(T.rsh[16 * k:16 * k + 16, 0:2 * H - o], T.sl[:, H + o:3 * H]).then_inc(S.lsh, 16)
+    for k in range(4):
+        t, o = 1 + k // 2, k % 2
+        A.dma_start(T.rsh[16 * k:16 * k + 16, 0:H - o], T.sl[:, H * t + o:H * t + H]).then_inc(S.lsh, 16)
+    for k in range(2):
+        group(A, "rpa", T.pa, k, "lpa")
     Y.wait_ge(S.mz, 1)
-    for k in range(8):
-        Y.dma_start(T.row[16 * k:16 * k + 1, :], T.pa[:, 0:2 * H]).then_inc(S.lrow, 16)
-    for k in range(2, 8):
-        group(Y, "rsl", T.sl, k, "ls2")
+    for k in range(4):
+        Y.dma_start(T.row[16 * k:16 * k + 1, :], T.pa[:, H * (k // 2):H * (k // 2) + 16]).then_inc(S.lrow, 16)
     load_x(1)
     load_w(0, 2)
-    for k in range(8):
-        group(Y, "rpa", T.pa, k, "lpa")
     load_x(2)
+    Y.wait_ge(S.q0, 1)
+    Y.dma_start(T.win0q[:, 0:C].bitcast(dt.uint8), T.k0q[:, :].bitcast(dt.uint8)).then_inc(S.cpq, 16)
+    Y.dma_start(T.win0s[:, 0:C], T.k0s[:, :]).then_inc(S.cps, 16)
+    load_x(3)
     behind(1)
     load_w(2, 4)
-    behind(2)
-    load_x(3)
 
     g.iota(T.ioJ[:, :], [[0, 3 * H]], 0, 1).then_inc(S.iot, 1)
     g.iota(T.ioK[:, :], [[0, R], [-16, H]], -NEW, 0).then_inc(S.iot, 1)
 
     waits = 0
     for t in rounds:
-        for part, where in CALLS[t]:
-            src, dst, i = T["sn%d%s" % (t, part)], T["win%d%s" % (t - 1, part)], "qs".index(part)
+        picked = []
+        for i, (part, to) in enumerate(calls[t]):
+            src, dst = T["sn%d%s" % (t, part)], T["win%d%s" % (t - 1, part)]
             trs, n = [], 0
-            for d in to[t][where]:
+            for d, es in to.items():
                 rid, pid = topo.addr(cores[d])[:2]
-                a, b = at[t][d], C + CAPP * r
+                a, b = CAPP * d, C + CAPP * r
                 sv, dv = src[:, a:a + CAPP], dst[:, b:b + CAPP]
                 if part == "q":
                     sv, dv = sv.bitcast(dt.uint8), dv.bitcast(dt.uint8)
                 sem = "an" + part if t == R and d in on else "ar%s%d" % (part, t)
-                trs.append(RemoteDMATransfer(dst_ids=[DstId(rid=rid, pnc=pid)], dma_engine_mask=bits(plan[t][d][i]),
+                trs.append(RemoteDMATransfer(dst_ids=[DstId(rid=rid, pnc=pid)], dma_engine_mask=bits(es),
                                              remote_sem=S[sem], srcs=[sv], dsts=[dv]))
-                n += len(plan[t][d][i])
-            first = t < R and (part, where) == CALLS[t][0]
-            waits += 0 if first else n
-            g.wait_ge(S["p%s%d%s" % (part, t, where)], 1)
-            g.remote_dma_fused(trs, local_sem=S["lq%d" % t] if first else S.left)
+                n += len(es)
+            waits += n
+            for k, (lo, hi) in enumerate(pieces[t]):
+                if (part, k) not in picked and any(lo <= d <= hi for d in to):
+                    picked.append((part, k))
+                    g.wait_ge(S["p%s%d%d" % (part, t, k)], 1)
+            g.remote_dma_fused(trs, local_sem=S.left)
+        if t != 2:
+            g.sem_inc(S["lq%d" % t], 1)
     g.wait_ge(S.left, waits)
 
     n = {"va": 0, "vb": 0}
@@ -181,123 +184,106 @@ def rank_program(g, core, T, topo):
             A.activation(T[out + "s"][:, o:o + w], T[win + "s"][:, 0:n_win].indirect(offs), ActivationFunctionType.Copy).then_inc(S[sem], 1)
 
     def pick_sends(part, t):
-        for w in PARTS:
-            a, b = min(at[t][d] for d in to[t][w]), max(at[t][d] for d in to[t][w]) + CAPP
+        turn = [min(to) for p, to in calls[t] if p == part]
+        for k, (lo, hi) in sorted(enumerate(pieces[t]), key=lambda e: turn.index(e[1][0])):
+            a, b = CAPP * lo, CAPP * hi + CAPP
             pick(part, "sn%d" % t, a, "k0" if t == 1 else "win%d" % (t - 2), C if t == 1 else WIN,
-                 T["o%d" % t][:, a // 16:b // 16], b - a, "p%s%d%s" % (part, t, w))
+                 T["o%d" % t][:, a // 16:b // 16], b - a, "p%s%d%d" % (part, t, k))
 
     def pick_cache(part, t):
         pick(part, "win%d" % t, 0, "win%d" % (t - 1), WIN, T.po[:, H * (t - 1):H * t], C, "k%s%d" % (part, t))
 
     def fill_own(part):
-        t = R - 1
-        pick(part, "win%d" % t, C + CAPP * r, "win%d" % (t - 1), WIN, T.po[:, H * (t - 1):H * (t - 1) + CAPP // 16], CAPP, "kf" + part)
+        pick(part, "win%d" % (R - 1), C + CAPP * r, "k0", C, T.o1[:, 0:CAPP // 16], CAPP, "kf" + part)
 
     def quantise(b, a, t, sem):
-        V.quantize_mx(T[b + "q"][:, a:a + C], T[b + "s"][:, a:a + C], T.xb[:, XP * t:XP * t + XP]).then_inc(S[sem], 1)
+        e = 2 if a == NEW and r == N - 1 and t < R else 0
+        V.quantize_mx(T[b + "q"][:, a - e:a + C], T[b + "s"][:, a - e:a + C], T.xb[:, XP * t - 4 * e:XP * t + XP]).then_inc(S[sem], 1)
 
     def quantise_w(a, b):
         V.wait_ge(S["lw%d" % a], 16)
         V.quantize_mx(T.wq[:, 128 * a:128 * b], T.ws[:, 128 * a:128 * b], T.wb[:, 512 * a:512 * b]).then_inc(S["qw%d" % a], 1)
 
+    one, two = slice(0, Q4), slice(0, 2 * Q4)
+
+    def spread(out, src, sem):
+        for k in range(4):
+            V.tensor_copy(out[Q4 * k:Q4 * k + Q4, :], src).then_inc(S[sem], 1)
+
     V.memset(T.row[:, :], 0).then_inc(S.mz, 1)
+    step("va", V.memset(T.ox[2 * Q4:, :], 0))
+    V.wait_ge(S.iot, 2)
+    step("vb", V.tensor_scalar(T.jl[one, :], T.ioJ[one, :], 15, None, AluOpType.bitwise_and))
+    need("vb")
+    step("vb", V.tensor_tensor(T.jt[one, :], T.ioK[one, :], T.jl[one, :], AluOpType.subtract))
     V.wait_ge(S.lsl, 32)
-    for k in range(4):
-        V.tensor_copy(T.o1[Q4 * k:Q4 * k + Q4, :], T.rsl[0:32, 0:H]).then_inc(S.o1r, 1)
+    spread(T.o1, T.rsl[one, 0:H], "o1r")
     V.wait_ge(S.lx0, 16)
     quantise("k0", 0, 0, "q0")
     V.wait_ge(S.o1r, 4)
     V.wait_ge(S.q0, 1)
     pick_sends("q", 1)
 
-    def gather(k):
-        need("va")
-        step("va", V.tensor_copy(T["m%d" % k][:, :], T.row[:, :].indirect(T.ox[:, H * k:H * k + H])))
+    V.wait_ge(S.lsh, 64)
+    def asked(k):
+        step("vb", V.tensor_scalar(T.tn[Q4 * k:Q4 * k + Q4, :], T.rsl[one, H * k + H:H * k + 2 * H], -1, -NEW, AluOpType.mult, AluOpType.add))
 
-    def turn(k):
-        need("va")
-        step("va", V.transpose(T["z%d" % k][:, :], T["m%d" % k][:, :]))
-
-    def fresh1(k):
-        need("va")
-        step("va", V.tensor_tensor(T["cu%d" % k][:, :], T["z%d" % k][:, 0:C:16], T.tn[:, H * k:H * k + H], AluOpType.mult))
-
-    def fresh2(k):
-        need("va")
-        step("va", V.tensor_tensor(T["cw%d" % k][:, :], T["cu%d" % k][:, :], T["z%d" % k][:, 0:C:16], AluOpType.max))
-
-    def offsets(k, out):
-        need("va")
-        for d, c, a in runs:
-            V.tensor_copy(T[out][:, a:a + 2 * c], T["cw%d" % k][:, 2 * d:2 * d + 2 * c]).then_inc(S[out + "r"], 1)
-
-    V.wait_ge(S.lsh, 128)
-    step("va", V.tensor_scalar(T.xh[:, :], T.rsh[:, 0:2 * H:2], 4, None, AluOpType.arith_shift_right))
-    for k in range(2):
-        step("va", V.tensor_scalar(T.xa[:, H // 2 * k:H // 2 * (k + 1)], T.rsh[:, H * k:H * k + H:2], 2 * H, H * k, AluOpType.mult, AluOpType.add))
-    V.wait_ge(S.ls2, 96)
-    step("vb", V.tensor_scalar(T.tp[:, :], T.rsl[:, H:3 * H], 0, NEW, AluOpType.max, AluOpType.add))
+    step("va", V.tensor_scalar(T.xa[two, :], T.rsh[two, 0:H:2], 257, None, AluOpType.mult))
+    asked(0)
     need("va")
-    step("va", V.tensor_scalar(T.xd[:, :], T.xh[:, :], 1 - 32 * H, None, AluOpType.mult))
-    quantise("win0", 0, 0, "nw0")
+    step("va", V.tensor_scalar(T.xc[two, :], T.xa[two, :], 4, 255, AluOpType.logical_shift_right, AluOpType.bitwise_and))
+    asked(1)
     need("va")
-    step("va", V.tensor_tensor(T.xc[:, :], T.xa[:, :], T.xd[:, :], AluOpType.add))
-    need("vb")
-    step("vb", V.tensor_scalar(T.tn[:, :], T.tp[:, :], -1, None, AluOpType.mult))
-    need("va")
-    step("va", V.tensor_copy(T.ox[:, 0:2 * H:2], T.xc[:, :]))
-    step("va", V.tensor_copy(T.ox[:, 1:2 * H:2], T.xc[:, :]))
+    step("va", V.tensor_copy(T.ox[two, 0:H:2], T.xc[two, :]))
+    step("va", V.tensor_copy(T.ox[two, 1:H:2], T.xc[two, :]))
     V.wait_ge(S.mz, 1)
-    V.wait_ge(S.lrow, 128)
-    gather(0)
+    V.wait_ge(S.lrow, 64)
+    need("va")
+    step("va", V.tensor_copy(T.m[:, :], T.row[:, :].indirect(T.ox[:, :])))
     V.wait_ge(S.lx1, 16)
     quantise("win0", NEW, 1, "nw0")
-    turn(0)
+    need("va")
+    step("va", V.transpose(T.z[two, :], T.m[two, :]))
     need("vb")
-    fresh1(0)
-    fresh2(0)
-    offsets(0, "o2")
+    need("va")
+    step("va", V.tensor_tensor(T.cu[two, :], T.z[two, 0:C:16], T.tn[two, :], AluOpType.mult))
+    need("va")
+    step("va", V.tensor_tensor(T.cw[two, :], T.cu[two, :], T.z[two, 0:C:16], AluOpType.max))
+    need("va")
+    spread(T.o2, T.cw[one, :], "o2r")
 
-    V.wait_ge(S.nw0, 2)
-    V.wait_ge(S.o2r, len(runs))
+    V.wait_ge(S.nw0, 1)
+    V.wait_ge(S.cpq, 16)
+    V.wait_ge(S.o2r, 4)
     V.wait_ge(S.arq1, arrive(1, "q", off + on))
     pick_sends("q", 2)
-    V.wait_ge(S.iot, 2)
-    step("vb", V.tensor_scalar(T.jl[:, :], T.ioJ[:, :], 15, None, AluOpType.bitwise_and))
-    gather(1)
+    V.wait_ge(S.lpa, 32)
+    step("vb", V.tensor_tensor(T.pu[one, :], T.rpa[one, :], T.jt[one, :], AluOpType.mult))
     need("vb")
-    step("vb", V.tensor_tensor(T.jt[:, :], T.ioK[:, :], T.jl[:, :], AluOpType.subtract))
-    turn(1)
-    V.wait_ge(S.lpa, 128)
+    step("vb", V.tensor_tensor(T.pr[one, :], T.pu[one, :], T.rpa[one, :], AluOpType.max))
+    spread(T.o3, T.cw[Q4:2 * Q4, :], "o3r")
     need("vb")
-    step("vb", V.tensor_tensor(T.pu[:, :], T.rpa[:, :], T.jt[:, :], AluOpType.mult))
-    fresh1(1)
-    need("vb")
-    step("vb", V.tensor_tensor(T.pr[:, :], T.pu[:, :], T.rpa[:, :], AluOpType.max))
-    fresh2(1)
-    need("vb")
-    V.tensor_copy(T.po[:, :], T.pr[:, :]).then_inc(S.por, 1)
-    offsets(1, "o3")
-    V.wait_ge(S.por, 1)
+    spread(T.po, T.pr[one, :], "por")
+    V.wait_ge(S.por, 4)
     pick_cache("q", 1)
     V.wait_ge(S.lx2, 16)
     quantise("win1", NEW, 2, "nw1")
 
     V.wait_ge(S.kq1, 1)
     V.wait_ge(S.nw1, 1)
-    V.wait_ge(S.o3r, len(runs))
+    V.wait_ge(S.o3r, 4)
     V.wait_ge(S.arq2, arrive(2, "q", off + on))
     pick_sends("q", 3)
+    quantise_w(0, 2)
     pick_cache("q", 2)
     fill_own("q")
-    quantise_w(0, 2)
     quantise_w(2, 4)
     V.wait_ge(S.lx3, 16)
     quantise("win2", NEW, 3, "nw2")
 
     home = sorted(on + [r])
     regions = {4: (NEW, NEW, C), 5: None, 6: None}
-    for bank, ranks in ((5, home), (6, off)):
+    for bank, ranks in ((5, home), (6, sorted(off))):
         a = C + CAPP * ranks[0]
         w = CAPP * len(ranks)
         regions[bank] = (a - (MIN - w) if a == C else a, a, w)
@@ -310,27 +296,32 @@ def rank_program(g, core, T, topo):
     h = H * (R - 1)
     V.tensor_copy(T.yb[:, R * C:R * C + C // 2], T.yw[:, :].indirect(T.po[:, h:h + H // 2])).then_inc(S.yc3, 1)
 
+    def result(t):
+        A.wait_ge(S["mm%d" % t], 1)
+        A.activation(T.yb[:, C * t:C * t + C], T.ps[:, BANK * t:BANK * t + C], ActivationFunctionType.Copy).then_inc(S["yc%d" % t], 1)
+
     A.wait_ge(S.o1r, 4)
     A.wait_ge(S.q0, 1)
     pick_sends("s", 1)
-    A.wait_ge(S.nw0, 2)
-    A.wait_ge(S.o2r, len(runs))
+    fill_own("s")
+    A.wait_ge(S.nw0, 1)
+    A.wait_ge(S.cps, 16)
+    A.wait_ge(S.o2r, 4)
     A.wait_ge(S.ars1, arrive(1, "s", off + on))
     pick_sends("s", 2)
-    A.wait_ge(S.por, 1)
+    A.wait_ge(S.por, 4)
     pick_cache("s", 1)
     A.wait_ge(S.ks1, 1)
     A.wait_ge(S.nw1, 1)
-    A.wait_ge(S.o3r, len(runs))
+    A.wait_ge(S.o3r, 4)
     A.wait_ge(S.ars2, arrive(2, "s", off + on))
     pick_sends("s", 3)
     pick_cache("s", 2)
-    fill_own("s")
-    for t in range(R):
-        A.wait_ge(S["mm%d" % t], 1)
-        A.activation(T.yb[:, C * t:C * t + C], T.ps[:, BANK * t:BANK * t + C], ActivationFunctionType.Copy).then_inc(S["yc%d" % t], 1)
+    result(0)
+    result(1)
     A.wait_ge(S.mm3, 1)
     A.activation(T.yw[:, 0:C], T.ps[:, BANK * 3:BANK * 3 + C], ActivationFunctionType.Copy).then_inc(S.ywr, 1)
+    result(2)
     A.wait_ge(S.ywr, 4)
     A.activation(T.yb[:, R * C + C // 2:R * C + C], T.yw[:, :].indirect(T.po[:, h + H // 2:h + H]), ActivationFunctionType.Copy).then_inc(S.yc3, 1)
 
@@ -350,8 +341,8 @@ def rank_program(g, core, T, topo):
     P.wait_ge(S.qw2, 1)
     P.wait_ge(S.kq2, 1)
     P.wait_ge(S.ks2, 1)
-    product(2, "win2", 0, C)
     product(3, "win2", 0, C)
+    product(2, "win2", 0, C)
     P.wait_ge(S.nw2, 1)
     product(4, "win2", NEW, C)
     P.wait_ge(S.kfq, 1)
@@ -363,7 +354,10 @@ def rank_program(g, core, T, topo):
     P.wait_ge(S.ars3, arrive(R, "s", off))
     product(6, "win2", regions[6][0], MIN)
 
-    for t in range(R + 1):
-        Y.wait_ge(S["yc%d" % t], 2 if t == R else 1)
-        Y.dma_start(T.y[:, C * t:C * t + C], T.yb[:, C * t:C * t + C]).then_inc(S.st, 16)
-    Y.wait_ge(S.st, 16 * (R + 1))
+    behind(R)
+    stores = ((0, 2), (2, 3), (3, 4))
+    for a, b in stores:
+        for t in range(a, b):
+            Y.wait_ge(S["yc%d" % t], 2 if t == R else 1)
+        Y.dma_start(T.y[:, C * a:C * b], T.yb[:, C * a:C * b]).then_inc(S.st, 16)
+    Y.wait_ge(S.st, 16 * len(stores))

from concourse.bass import DstId, RemoteDMATransfer
from concourse.mybir import dt, AluOpType, ActivationFunctionType

C, R, CAPP, N = 192, 3, 32, 6
WIN = 3 * C
NEW = 2 * C
H = C // 16
Q4 = 128 // 4
MIN = 128
BANK = 512

CODE, PLANE = "float8_e4m3fn_x4", "uint8"
SCRATCH = {
    "xb": ("sbuf", [128, 4 * C * (R + 1)], "bfloat16"),
    "wb": ("sbuf", [128, 512 * (R + 1)], "bfloat16"),
    "wq": ("sbuf", [128, 128 * (R + 1)], CODE), "ws": ("sbuf", [128, 128 * (R + 1)], PLANE),
    "k0q": ("sbuf", [128, C], CODE), "k0s": ("sbuf", [128, C], PLANE),
    "yb": ("sbuf", [128, C * (R + 1)], "float32"), "yw": ("sbuf", [128, WIN], "float32"),
    "ps": ("psum", [128, BANK * 7], "float32"),
    "rsl": ("sbuf", [128, 3 * H], "int32"), "rpa": ("sbuf", [128, 3 * H], "int32"),
    "rsh": ("sbuf", [128, H], "int32"), "row": ("sbuf", [128, 256], "int32"),
    "xa": ("sbuf", [128, H // 2], "int32"), "xc": ("sbuf", [128, H // 2], "int32"), "ox": ("sbuf", [128, H], "uint16"),
    "tn": ("sbuf", [128, H], "float32"), "m": ("sbuf", [128, C], "float32"), "z": ("sbuf", [128, C], "float32"),
    "cu": ("sbuf", [128, H], "float32"), "cw": ("sbuf", [128, H], "float32"),
    "ioJ": ("sbuf", [128, 3 * H], "int32"), "ioK": ("sbuf", [128, 3 * H], "int32"),
    "jl": ("sbuf", [128, 3 * H], "int32"), "jt": ("sbuf", [128, 3 * H], "int32"),
    "pu": ("sbuf", [128, 3 * H], "int32"), "pr": ("sbuf", [128, 3 * H], "int32"),
    "o1": ("sbuf", [128, H], "uint16"), "o2": ("sbuf", [128, H], "uint16"), "o3": ("sbuf", [128, H], "uint16"),
    "po": ("sbuf", [128, 3 * H], "uint16"),
}
for _t in range(R):
    SCRATCH["win%dq" % _t] = ("sbuf", [128, WIN], CODE)
    SCRATCH["win%ds" % _t] = ("sbuf", [128, WIN], PLANE)
    SCRATCH["sn%dq" % (_t + 1)] = ("sbuf", [128, C], CODE)
    SCRATCH["sn%ds" % (_t + 1)] = ("sbuf", [128, C], PLANE)

SEMAPHORES = (["lx0", "lx1", "lx2", "lx3", "lw0", "lw2", "lsl", "cpq", "cps", "lsh", "lpa", "lrow", "st", "mz", "iot",
               "va", "vb", "o1r", "o2r", "o3r", "por", "q0", "nw0", "nw1", "nw2", "qw0", "qw2", "lq1", "lq3", "left",
               "kfq", "kfs", "anq", "ans", "ywr"]
              + ["%s%d" % (n, t) for t in (1, 2, 3) for n in ("kq", "ks", "arq", "ars")]
              + ["p%s%d%d" % (n, t, w) for t in (1, 2, 3) for n in "qs" for w in range(N - 1)]
              + ["mm%d" % t for t in range(7)] + ["yc%d" % t for t in range(4)])


def peers(topo, cores, r):
    ds = [d for d in range(len(cores)) if d != r]
    home = topo.chip(cores[r])
    return [d for d in ds if topo.chip(cores[d]) != home], [d for d in ds if topo.chip(cores[d]) == home]


def bits(es):
    return sum(1 << e for e in es)


def share(ds, es):
    k = len(es) // len(ds)
    return {d: es[k * i:k * i + k] for i, d in enumerate(ds)}


def lone(topo, cores, r):
    return [(topo.chip(c), topo.die(c)) for c in cores].count((topo.chip(cores[r]), topo.die(cores[r]))) == 1


def calls_of(topo, cores, r, t):
    off, on = peers(topo, cores, r)
    far = topo.engines(cores[r], cores[off[0]])
    near = [e for e in topo.engines(cores[r], cores[on[0]]) if e not in far]
    n = share(on, near)
    i = sorted(on + [r]).index(r) + 1
    off = off[i % len(off):] + off[:i % len(off)]
    if t < R and not lone(topo, cores, r):
        off.sort(key=lambda d: (lone(topo, cores, d), d))
        off.insert(1, off.pop())
    a, b, c = [{d: far} for d in off]
    on.sort(key=lambda d: topo.die(cores[d]) == topo.die(cores[r]))
    u, v = [{d: near} for d in on]
    if t == 1:
        if lone(topo, cores, r):
            return [(part, to) for part in "qs" for to in (a, b, n, c)]
        return [("q", to) for to in (a, b, c, n)] + [("s", to) for to in (b, c, a, n)]
    if t < R and not lone(topo, cores, r):
        return [("q", to) for to in (a, u, b, c, v)] + [("s", to) for to in (b, u, c, a, v)]
    if t == R and r > max(on):
        return [("q", a), ("q", u), ("q", b), ("q", v), ("s", a), ("q", c), ("s", u), ("s", b), ("s", c), ("s", v)]
    return [(part, to) for part in "qs" for to in ((a, u, b, v, c) if lone(topo, cores, r) else (a, u, b, c, v))]


def pieces_of(calls, t):
    return [(min(to), max(to)) for part, to in calls if part == "q"]


def rank_program(g, core, T, topo):
    r = T.rank_of(core)
    if r is None:
        return
    S, V, A, Y = T.sem, g.vector, g.scalar, g.sync
    cores = list(T.cores)
    rounds = range(1, R + 1)
    off, on = peers(topo, cores, r)
    calls = {t: calls_of(topo, cores, r, t) for t in rounds}
    pieces = {t: pieces_of(calls[t], t) for t in rounds}

    def arrive(t, part, sources):
        return sum(len(to[r]) for q in sources for p, to in calls_of(topo, cores, q, t) if p == part and r in to)

    XP = 4 * C

    def load_x(t):
        Y.dma_start(T.xb[:, XP * t:XP * t + XP], T.x[:, XP * t:XP * t + XP]).then_inc(S["lx%d" % t], 16)

    def load_w(a, b):
        Y.dma_start(T.wb[:, 512 * a:512 * b], T.w[:, 512 * a:512 * b]).then_inc(S["lw%d" % a], 16)

    def group(queue, buf, src, k, sem):
        queue.dma_start(T[buf][16 * k:16 * k + 16, :], src[:, :]).then_inc(S[sem], 16)

    def behind(t):
        Y.wait_ge(S["lq%d" % t], 1)

    load_x(0)
    group(A, "rsl", T.sl, 0, "lsl")
    group(A, "rsl", T.sl, 1, "lsl")
    for k in range(4):
        t, o = 1 + k // 2, k % 2
        A.dma_start(T.rsh[16 * k:16 * k + 16, 0:H - o], T.sl[:, H * t + o:H * t + H]).then_inc(S.lsh, 16)
    for k in range(2):
        group(A, "rpa", T.pa, k, "lpa")
    Y.wait_ge(S.mz, 1)
    for k in range(4):
        Y.dma_start(T.row[16 * k:16 * k + 1, :], T.pa[:, H * (k // 2):H * (k // 2) + 16]).then_inc(S.lrow, 16)
    load_x(1)
    load_w(0, 2)
    load_x(2)
    Y.wait_ge(S.q0, 1)
    Y.dma_start(T.win0q[:, 0:C].bitcast(dt.uint8), T.k0q[:, :].bitcast(dt.uint8)).then_inc(S.cpq, 16)
    Y.dma_start(T.win0s[:, 0:C], T.k0s[:, :]).then_inc(S.cps, 16)
    load_x(3)
    behind(1)
    load_w(2, 4)

    g.iota(T.ioJ[:, :], [[0, 3 * H]], 0, 1).then_inc(S.iot, 1)
    g.iota(T.ioK[:, :], [[0, R], [-16, H]], -NEW, 0).then_inc(S.iot, 1)

    waits = 0
    for t in rounds:
        picked = []
        for i, (part, to) in enumerate(calls[t]):
            src, dst = T["sn%d%s" % (t, part)], T["win%d%s" % (t - 1, part)]
            trs, n = [], 0
            for d, es in to.items():
                rid, pid = topo.addr(cores[d])[:2]
                a, b = CAPP * d, C + CAPP * r
                sv, dv = src[:, a:a + CAPP], dst[:, b:b + CAPP]
                if part == "q":
                    sv, dv = sv.bitcast(dt.uint8), dv.bitcast(dt.uint8)
                sem = "an" + part if t == R and d in on else "ar%s%d" % (part, t)
                trs.append(RemoteDMATransfer(dst_ids=[DstId(rid=rid, pnc=pid)], dma_engine_mask=bits(es),
                                             remote_sem=S[sem], srcs=[sv], dsts=[dv]))
                n += len(es)
            waits += n
            for k, (lo, hi) in enumerate(pieces[t]):
                if (part, k) not in picked and any(lo <= d <= hi for d in to):
                    picked.append((part, k))
                    g.wait_ge(S["p%s%d%d" % (part, t, k)], 1)
            g.remote_dma_fused(trs, local_sem=S.left)
        if t != 2:
            g.sem_inc(S["lq%d" % t], 1)
    g.wait_ge(S.left, waits)

    n = {"va": 0, "vb": 0}

    def step(chain, call):
        call.then_inc(S[chain], 1)
        n[chain] += 1

    def need(chain):
        V.wait_ge(S[chain], n[chain])

    def pick(part, out, o, win, n_win, offs, w, sem):
        if part == "q":
            V.tensor_copy(T[out + "q"][:, o:o + w].bitcast(dt.uint32),
                          T[win + "q"][:, 0:n_win].bitcast(dt.uint32).indirect(offs)).then_inc(S[sem], 1)
        else:
            A.activation(T[out + "s"][:, o:o + w], T[win + "s"][:, 0:n_win].indirect(offs), ActivationFunctionType.Copy).then_inc(S[sem], 1)

    def pick_sends(part, t):
        turn = [min(to) for p, to in calls[t] if p == part]
        for k, (lo, hi) in sorted(enumerate(pieces[t]), key=lambda e: turn.index(e[1][0])):
            a, b = CAPP * lo, CAPP * hi + CAPP
            pick(part, "sn%d" % t, a, "k0" if t == 1 else "win%d" % (t - 2), C if t == 1 else WIN,
                 T["o%d" % t][:, a // 16:b // 16], b - a, "p%s%d%d" % (part, t, k))

    def pick_cache(part, t):
        pick(part, "win%d" % t, 0, "win%d" % (t - 1), WIN, T.po[:, H * (t - 1):H * t], C, "k%s%d" % (part, t))

    def fill_own(part):
        pick(part, "win%d" % (R - 1), C + CAPP * r, "k0", C, T.o1[:, 0:CAPP // 16], CAPP, "kf" + part)

    def quantise(b, a, t, sem):
        e = 2 if a == NEW and r == N - 1 and t < R else 0
        V.quantize_mx(T[b + "q"][:, a - e:a + C], T[b + "s"][:, a - e:a + C], T.xb[:, XP * t - 4 * e:XP * t + XP]).then_inc(S[sem], 1)

    def quantise_w(a, b):
        V.wait_ge(S["lw%d" % a], 16)
        V.quantize_mx(T.wq[:, 128 * a:128 * b], T.ws[:, 128 * a:128 * b], T.wb[:, 512 * a:512 * b]).then_inc(S["qw%d" % a], 1)

    one, two = slice(0, Q4), slice(0, 2 * Q4)

    def spread(out, src, sem):
        for k in range(4):
            V.tensor_copy(out[Q4 * k:Q4 * k + Q4, :], src).then_inc(S[sem], 1)

    V.memset(T.row[:, :], 0).then_inc(S.mz, 1)
    step("va", V.memset(T.ox[2 * Q4:, :], 0))
    V.wait_ge(S.iot, 2)
    step("vb", V.tensor_scalar(T.jl[one, :], T.ioJ[one, :], 15, None, AluOpType.bitwise_and))
    need("vb")
    step("vb", V.tensor_tensor(T.jt[one, :], T.ioK[one, :], T.jl[one, :], AluOpType.subtract))
    V.wait_ge(S.lsl, 32)
    spread(T.o1, T.rsl[one, 0:H], "o1r")
    V.wait_ge(S.lx0, 16)
    quantise("k0", 0, 0, "q0")
    V.wait_ge(S.o1r, 4)
    V.wait_ge(S.q0, 1)
    pick_sends("q", 1)

    V.wait_ge(S.lsh, 64)
    def asked(k):
        step("vb", V.tensor_scalar(T.tn[Q4 * k:Q4 * k + Q4, :], T.rsl[one, H * k + H:H * k + 2 * H], -1, -NEW, AluOpType.mult, AluOpType.add))

    step("va", V.tensor_scalar(T.xa[two, :], T.rsh[two, 0:H:2], 257, None, AluOpType.mult))
    asked(0)
    need("va")
    step("va", V.tensor_scalar(T.xc[two, :], T.xa[two, :], 4, 255, AluOpType.logical_shift_right, AluOpType.bitwise_and))
    asked(1)
    need("va")
    step("va", V.tensor_copy(T.ox[two, 0:H:2], T.xc[two, :]))
    step("va", V.tensor_copy(T.ox[two, 1:H:2], T.xc[two, :]))
    V.wait_ge(S.mz, 1)
    V.wait_ge(S.lrow, 64)
    need("va")
    step("va", V.tensor_copy(T.m[:, :], T.row[:, :].indirect(T.ox[:, :])))
    V.wait_ge(S.lx1, 16)
    quantise("win0", NEW, 1, "nw0")
    need("va")
    step("va", V.transpose(T.z[two, :], T.m[two, :]))
    need("vb")
    need("va")
    step("va", V.tensor_tensor(T.cu[two, :], T.z[two, 0:C:16], T.tn[two, :], AluOpType.mult))
    need("va")
    step("va", V.tensor_tensor(T.cw[two, :], T.cu[two, :], T.z[two, 0:C:16], AluOpType.max))
    need("va")
    spread(T.o2, T.cw[one, :], "o2r")

    V.wait_ge(S.nw0, 1)
    V.wait_ge(S.cpq, 16)
    V.wait_ge(S.o2r, 4)
    V.wait_ge(S.arq1, arrive(1, "q", off + on))
    pick_sends("q", 2)
    V.wait_ge(S.lpa, 32)
    step("vb", V.tensor_tensor(T.pu[one, :], T.rpa[one, :], T.jt[one, :], AluOpType.mult))
    need("vb")
    step("vb", V.tensor_tensor(T.pr[one, :], T.pu[one, :], T.rpa[one, :], AluOpType.max))
    spread(T.o3, T.cw[Q4:2 * Q4, :], "o3r")
    need("vb")
    spread(T.po, T.pr[one, :], "por")
    V.wait_ge(S.por, 4)
    pick_cache("q", 1)
    V.wait_ge(S.lx2, 16)
    quantise("win1", NEW, 2, "nw1")

    V.wait_ge(S.kq1, 1)
    V.wait_ge(S.nw1, 1)
    V.wait_ge(S.o3r, 4)
    V.wait_ge(S.arq2, arrive(2, "q", off + on))
    pick_sends("q", 3)
    quantise_w(0, 2)
    pick_cache("q", 2)
    fill_own("q")
    quantise_w(2, 4)
    V.wait_ge(S.lx3, 16)
    quantise("win2", NEW, 3, "nw2")

    home = sorted(on + [r])
    regions = {4: (NEW, NEW, C), 5: None, 6: None}
    for bank, ranks in ((5, home), (6, sorted(off))):
        a = C + CAPP * ranks[0]
        w = CAPP * len(ranks)
        regions[bank] = (a - (MIN - w) if a == C else a, a, w)

    for bank in (4, 5, 6):
        s, a, w = regions[bank]
        V.wait_ge(S["mm%d" % bank], 1)
        V.tensor_copy(T.yw[:, a:a + w], T.ps[:, BANK * bank + a - s:BANK * bank + a - s + w]).then_inc(S.ywr, 1)
    V.wait_ge(S.ywr, 4)
    h = H * (R - 1)
    V.tensor_copy(T.yb[:, R * C:R * C + C // 2], T.yw[:, :].indirect(T.po[:, h:h + H // 2])).then_inc(S.yc3, 1)

    def result(t):
        A.wait_ge(S["mm%d" % t], 1)
        A.activation(T.yb[:, C * t:C * t + C], T.ps[:, BANK * t:BANK * t + C], ActivationFunctionType.Copy).then_inc(S["yc%d" % t], 1)

    A.wait_ge(S.o1r, 4)
    A.wait_ge(S.q0, 1)
    pick_sends("s", 1)
    fill_own("s")
    A.wait_ge(S.nw0, 1)
    A.wait_ge(S.cps, 16)
    A.wait_ge(S.o2r, 4)
    A.wait_ge(S.ars1, arrive(1, "s", off + on))
    pick_sends("s", 2)
    A.wait_ge(S.por, 4)
    pick_cache("s", 1)
    A.wait_ge(S.ks1, 1)
    A.wait_ge(S.nw1, 1)
    A.wait_ge(S.o3r, 4)
    A.wait_ge(S.ars2, arrive(2, "s", off + on))
    pick_sends("s", 3)
    pick_cache("s", 2)
    result(0)
    result(1)
    A.wait_ge(S.mm3, 1)
    A.activation(T.yw[:, 0:C], T.ps[:, BANK * 3:BANK * 3 + C], ActivationFunctionType.Copy).then_inc(S.ywr, 1)
    result(2)
    A.wait_ge(S.ywr, 4)
    A.activation(T.yb[:, R * C + C // 2:R * C + C], T.yw[:, :].indirect(T.po[:, h + H // 2:h + H]), ActivationFunctionType.Copy).then_inc(S.yc3, 1)

    P = g.tensor

    def product(bank, b, a, w):
        t = min(bank, R)
        P.matmul_mx(T.ps[:, BANK * bank:BANK * bank + w], T.wq[:, 128 * t:128 * t + 128], T.ws[:, 128 * t:128 * t + 128],
                    T[b + "q"][:, a:a + w], T[b + "s"][:, a:a + w], True, True).then_inc(S["mm%d" % bank], 1)

    P.wait_ge(S.q0, 1)
    P.wait_ge(S.qw0, 1)
    product(0, "k0", 0, C)
    P.wait_ge(S.kq1, 1)
    P.wait_ge(S.ks1, 1)
    product(1, "win1", 0, C)
    P.wait_ge(S.qw2, 1)
    P.wait_ge(S.kq2, 1)
    P.wait_ge(S.ks2, 1)
    product(3, "win2", 0, C)
    product(2, "win2", 0, C)
    P.wait_ge(S.nw2, 1)
    product(4, "win2", NEW, C)
    P.wait_ge(S.kfq, 1)
    P.wait_ge(S.kfs, 1)
    P.wait_ge(S.anq, arrive(R, "q", on))
    P.wait_ge(S.ans, arrive(R, "s", on))
    product(5, "win2", regions[5][0], MIN)
    P.wait_ge(S.arq3, arrive(R, "q", off))
    P.wait_ge(S.ars3, arrive(R, "s", off))
    product(6, "win2", regions[6][0], MIN)

    behind(R)
    stores = ((0, 2), (2, 3), (3, 4))
    for a, b in stores:
        for t in range(a, b):
            Y.wait_ge(S["yc%d" % t], 2 if t == R else 1)
        Y.dma_start(T.y[:, C * a:C * b], T.yb[:, C * a:C * b]).then_inc(S.st, 16)
    Y.wait_ge(S.st, 16 * len(stores))
